import numpy as np
import ml_dtypes


def mxq(x, axis, fmt="e4m3"):
    dtype, down = {"e4m3": (ml_dtypes.float8_e4m3fn, 7), "e5m2": (ml_dtypes.float8_e5m2, 14)}[fmt]
    v = np.moveaxis(np.asarray(x, np.float32).astype(ml_dtypes.bfloat16).astype(np.float64), axis, -1)
    blocks = v.reshape(v.shape[:-1] + (-1, 32))
    amax = np.abs(blocks).max(-1, keepdims=True)
    byte = np.maximum(np.where(amax > 0, np.frexp(amax)[1] - 1 + 127, 0) - down, 1)
    scale = np.exp2(byte - 127.0)
    codes = (blocks / scale).astype(np.float32).astype(dtype).astype(np.float64)
    return np.moveaxis((codes * scale).reshape(v.shape), -1, axis)


WIDE = False


def mx_kscale(k):
    if not WIDE:
        return np.ones(k)
    levels = np.array([10, -10, 5, -5, 0])
    if k % 512:
        return np.exp2(np.random.permutation(np.resize(levels, k // 32))).repeat(32)
    a = np.empty((k // 512, 16))
    for p in range(k // 512):
        a[p, :8] = np.random.permutation(np.resize(levels, 8))
        for g in range(8):
            far = levels[np.abs(levels - a[p, g]) >= 10]
            a[p, g + 8] = far[np.random.randint(len(far))]
    return np.exp2(a.ravel()).repeat(32)


def f64(x):
    return np.asarray(x).astype(np.float64)


def striped(idx):
    return np.tile(np.asarray(idx).reshape(-1, 16).T, (8, 1)).astype(np.uint16)


def unstriped(offs):
    return offs[:16].T.reshape(-1).astype(np.int64)


E2M1 = np.array([0.0, 0.5, 1.0, 1.5, 2.0, 3.0, 4.0, 6.0, -0.0, -0.5, -1.0, -1.5, -2.0, -3.0, -4.0, -6.0])


def pack_weight(w, fmt):
    k, n = w.shape
    w = f64(np.asarray(w, np.float32).astype(ml_dtypes.bfloat16)).reshape(k // 32, 32, n)
    amax = np.abs(w).max(1)
    if fmt == "e4m3":
        byte = np.frexp(amax)[1] - 1 + 127 - 7
    else:
        mant, ex = np.frexp(amax / 6.0)
        byte = np.where(mant > 0.5, ex, ex - 1) + 127
    byte = np.clip(np.where(amax > 0, byte, 1), 1, 254)
    scaled = (w * np.exp2(127.0 - byte)[:, None, :]).reshape(k, n).astype(np.float32)
    by_word = np.ascontiguousarray(scaled.reshape(k // 512, 128, 4, n).transpose(0, 1, 3, 2))
    if fmt == "e4m3":
        words = by_word.astype(ml_dtypes.float8_e4m3fn).view(np.uint8)
    else:
        c = by_word.astype(ml_dtypes.float4_e2m1fn).view(np.uint8) & 0xF
        words = (c[..., 0::2] | (c[..., 1::2] << 4)).reshape(k // 512, 128, 2 * n)
    return np.ascontiguousarray(words), np.ascontiguousarray(byte.astype(np.uint8).reshape(k // 512, 16, n))


def unpack_weight(words, scales, fmt):
    g, _, n = scales.shape
    words = np.ascontiguousarray(words).reshape(g, 128, n, -1)
    if fmt == "e4m3":
        vals = words.view(ml_dtypes.float8_e4m3fn).astype(np.float64)
    else:
        nib = np.empty((g, 128, n, 4), np.uint8)
        nib[..., 0::2] = words & 0xF
        nib[..., 1::2] = words >> 4
        vals = E2M1[nib]
    vals = vals * np.repeat(np.exp2(scales.astype(np.float64) - 127.0), 8, axis=1)[..., None]
    return vals.transpose(0, 1, 3, 2).reshape(g * 512, n)


D, T, I, J, U, Z, M, N = 512, 2048, 512, 512, 1024, 1024, 512, 64


def setup_inputs():
    n = np.random.standard_normal
    idx = np.random.permutation(T)[:I]
    idx2 = np.random.permutation(U)[:J]
    idx3 = np.random.permutation(Z)[:J]
    idx4 = np.random.permutation(M)[:N]
    fd = mx_kscale(D)
    keysp = pack_weight(n((D, T)) / fd[:, None], "e4m3")
    return {
        "keys_words": keysp[0],
        "keys_scales": keysp[1],
        "notes": (n((D, U)) * 1.0 / np.sqrt(D) * fd[:, None]).astype(np.float32),
        "users2": (n((D, Z)) * 1.0 / np.sqrt(D) * fd[:, None]).astype(np.float32),
        "old": (1.0 * n((I, M))).astype(np.float32),
        "offs": striped(idx),
        "offs2": striped(idx2),
        "offs3": striped(idx3),
        "offs4": striped(idx4),
    }


def reference(keys_words, keys_scales, notes, users2, old, offs, offs2, offs3, offs4):
    idx = unstriped(offs)
    idx2 = unstriped(offs2)
    idx3 = unstriped(offs3)
    idx4 = unstriped(offs4)
    keysu = unpack_weight(keys_words, keys_scales, "e4m3")
    keysidxg = keysu[:, idx]
    notesidx2q = mxq(f64(notes)[:, idx2], 0, "e4m3")
    g1 = keysidxg.T @ notesidx2q
    users2idx3q = mxq(f64(users2)[:, idx3], 0, "e4m3")
    g2 = keysidxg.T @ users2idx3q
    g0 = np.maximum(g1, g2)
    rb0 = g0.reshape(I, N, J // N).max(axis=2)
    gf = np.zeros((I, M))
    gf[:, idx4] = rb0
    y = f64(old) + gf
    return y

@@ -1,0 +1,134 @@
+from contextlib import ExitStack
+
+import concourse.mybir as mybir
+
+D, T, I, J, U, M, N = 512, 2048, 512, 512, 1024, 512, 64
+FLOPS = 2 * 2 * D * I * J
+
+F32 = mybir.dt.float32
+BF16 = mybir.dt.bfloat16
+I32 = mybir.dt.int32
+U32 = mybir.dt.uint32
+U16 = mybir.dt.uint16
+U8 = mybir.dt.uint8
+FP8X4 = mybir.dt.float8_e4m3fn_x4
+COPY = mybir.ActivationFunctionType.Copy
+MAX = mybir.AluOpType.max
+ADD = mybir.AluOpType.add
+AXIS_X = mybir.AxisListType.X
+
+P = 128
+PACK = 4
+RUN = J // N
+TILES = I // P
+HALF = J // 2
+
+
+def tile_attend_tab_larger_runsput_kernel(tc, keys_words, keys_scales, notes, users2, old, offs, offs2, offs3, offs4, out):
+    nc = tc.nc
+    with ExitStack() as ctx:
+        sb = ctx.enter_context(tc.tile_pool(name="sb", bufs=1))
+        ps = ctx.enter_context(tc.psum_pool(name="ps", bufs=1))
+
+        l_keys = sb.tile([P, I // 16], U16, name="l_keys")
+        l_notes = sb.tile([P, J // 16], U16, name="l_notes")
+        l_users = sb.tile([P, J // 16], U16, name="l_users")
+        l_put = sb.tile([P, N // 16], U16, name="l_put")
+        kw = sb.tile([P, T], I32, name="kw")
+        ks = sb.tile([P, T], U8, name="ks")
+        npl = [sb.tile([P, U], F32, name="npl%d" % t) for t in range(PACK)]
+        upl = [sb.tile([P, U], F32, name="upl%d" % t) for t in range(PACK)]
+        olds = [sb.tile([P, M], F32, name="old%d" % r) for r in range(TILES)]
+        puts = [sb.tile([P, M], F32, name="put%d" % r) for r in range(TILES)]
+
+        nc.vector.memset(ks[:].bitcast(I32), 0)
+        for r in range(TILES):
+            nc.gpsimd.memset(puts[r][:], 0.0)
+
+        nv = notes.rearrange("(p t) u -> p t u", t=PACK)
+        uv = users2.rearrange("(p t) u -> p t u", t=PACK)
+        nc.sync.dma_start(npl[0][:], nv[:, 0, :])
+        nc.sync.dma_start(l_notes[:], offs2)
+        nc.sync.dma_start(l_keys[:], offs)
+        for q in range(4):
+            nc.scalar.dma_start(ks[32 * q : 32 * q + 4, :].bitcast(I32), keys_scales[0, 4 * q : 4 * q + 4, :].bitcast(I32))
+        for t in range(1, PACK):
+            nc.sync.dma_start(npl[t][:], nv[:, t, :])
+        nc.sync.dma_start(kw[:], keys_words[0].rearrange("p n t -> p (n t)").bitcast(I32))
+        nc.sync.dma_start(l_users[:], offs3)
+        nc.sync.dma_start(l_put[:], offs4)
+        for t in range(PACK):
+            nc.sync.dma_start(upl[t][:], uv[:, t, :])
+        for r in range(TILES):
+            nc.sync.dma_start(olds[r][:], old[r * P : (r + 1) * P, :])
+
+        def gather(engine, dst, plane, offsets):
+            if engine == "v":
+                nc.vector.tensor_copy(dst, plane[:].indirect(offsets))
+            else:
+                nc.scalar.activation(dst, plane[:].indirect(offsets), COPY)
+
+        def weave(dst, src):
+            nc.vector.tensor_copy(
+                dst[:].rearrange("p (c i) t -> p c t i", i=4),
+                src.rearrange("p t (c i) -> p c t i", i=4),
+            )
+
+        ng = sb.tile([P, PACK, J], BF16, name="ng")
+        for t in range(PACK):
+            gather("vs"[t % 2], ng[:, t, :], npl[t], l_notes[:])
+        kq_s = sb.tile([P, I], U8, name="kq_s", align_bytes=64)
+        nc.vector.tensor_copy(kq_s[:], ks[:].indirect(l_keys[:]))
+        nw = sb.tile([P, J, PACK], BF16, name="nw", align_bytes=64)
+        weave(nw, ng[:])
+        nq = sb.tile([P, J], U32, name="nq", align_bytes=64)
+        nq_s = sb.tile([P, J], U8, name="nq_s", align_bytes=64)
+        nc.vector.quantize_mx(out=nq[:].bitcast(FP8X4), scales=nq_s[:], in_=nw[:].rearrange("p c t -> p (c t)"))
+
+        kq = [sb.tile([P, P], U32, name="kq%d" % r, align_bytes=64) for r in range(TILES)]
+        best = [sb.tile([P, 2, N], F32, name="best%d" % r) for r in range(TILES)]
+        g1 = [ps.tile([P, J], F32, name="g1_%d" % r) for r in range(TILES)]
+        g2 = [ps.tile([P, J], F32, name="g2_%d" % r) for r in range(TILES)]
+        for r in range(TILES):
+            nc.vector.tensor_copy(kq[r][:], kw[:].bitcast(U32).indirect(l_keys[:, 8 * r : 8 * r + 8]))
+            nc.tensor.matmul_mx(
+                out=g1[r][:], lhsT=kq[r][:].bitcast(FP8X4), lhsT_scale=kq_s[:, r * P : (r + 1) * P],
+                rhs=nq[:].bitcast(FP8X4), rhs_scale=nq_s[:], start=True, stop=True,
+            )
+        for r in range(TILES):
+            nc.vector.tensor_reduce(best[r][:, 0, :], g1[r][:].rearrange("p (n e) -> p n e", e=RUN), AXIS_X, MAX)
+
+        ug = sb.tile([P, PACK, J], BF16, name="ug")
+        for t in range(PACK - 1):
+            gather("s", ug[:, t, :], upl[t], l_users[:])
+        gather("v", ug[:, 3, 0:HALF], upl[3], l_users[:, 0:16])
+        gather("s", ug[:, 3, HALF:J], upl[3], l_users[:, 16:32])
+        uw = [sb.tile([P, HALF, PACK], BF16, name="uw%d" % h, align_bytes=64) for h in range(2)]
+        uq = [sb.tile([P, HALF], U32, name="uq%d" % h, align_bytes=64) for h in range(2)]
+        uq_s = [sb.tile([P, HALF], U8, name="uq_s%d" % h, align_bytes=64) for h in range(2)]
+        for h in range(2):
+            weave(uw[h], ug[:, :, h * HALF : (h + 1) * HALF])
+        for h in range(2):
+            nc.vector.quantize_mx(out=uq[h][:].bitcast(FP8X4), scales=uq_s[h][:], in_=uw[h][:].rearrange("p c t -> p (c t)"))
+        for r in range(TILES):
+            for h in range(2):
+                nc.tensor.matmul_mx(
+                    out=g2[r][:, h * HALF : (h + 1) * HALF], lhsT=kq[r][:].bitcast(FP8X4), lhsT_scale=kq_s[:, r * P : (r + 1) * P],
+                    rhs=uq[h][:].bitcast(FP8X4), rhs_scale=uq_s[h][:], start=True, stop=True,
+                )
+
+        rb = [sb.tile([P, N], F32, name="rb%d" % r) for r in range(TILES)]
+        res = [sb.tile([P, M], F32, name="res%d" % r) for r in range(TILES)]
+
+        def finish(r):
+            nc.vector.tensor_reduce(rb[r][:], best[r][:].rearrange("p s n -> p n s"), AXIS_X, MAX)
+            nc.scalar.activation(puts[r][:].indirect(l_put[:]), rb[r][:], COPY)
+
+        for r in range(TILES):
+            nc.vector.tensor_reduce(best[r][:, 1, :], g2[r][:].rearrange("p (n e) -> p n e", e=RUN), AXIS_X, MAX)
+            if r > 0:
+                finish(r - 1)
+        finish(TILES - 1)
+        for r in range(TILES):
+            nc.vector.tensor_tensor(res[r][:], puts[r][:], olds[r][:], ADD)
+            nc.sync.dma_start(out[r * P : (r + 1) * P, :], res[r][:])

@@ -15,7 +15,7 @@ FP8X4 = mybir.dt.float8_e4m3fn_x4
 COPY = mybir.ActivationFunctionType.Copy
 MAX = mybir.AluOpType.max
 ADD = mybir.AluOpType.add
-AXIS_X = mybir.AxisListType.X
+AXIS_XY = mybir.AxisListType.XY
 
 P = 128
 PACK = 4
@@ -41,7 +41,9 @@ def tile_attend_tab_larger_runsput_kernel(tc, keys_words, keys_scales, notes, us
         olds = [sb.tile([P, M], F32, name="old%d" % r) for r in range(TILES)]
         puts = [sb.tile([P, M], F32, name="put%d" % r) for r in range(TILES)]
 
-        nc.vector.memset(ks[:].bitcast(I32), 0)
+        nc.gpsimd.memset(ks[:].bitcast(I32), 0)
+        for q in range(4):
+            nc.gpsimd.dma_start(ks[32 * q : 32 * q + 4, :].bitcast(I32), keys_scales[0, 4 * q : 4 * q + 4, :].bitcast(I32))
         for r in range(TILES):
             nc.gpsimd.memset(puts[r][:], 0.0)
 
@@ -50,85 +52,80 @@ def tile_attend_tab_larger_runsput_kernel(tc, keys_words, keys_scales, notes, us
         nc.sync.dma_start(npl[0][:], nv[:, 0, :])
         nc.sync.dma_start(l_notes[:], offs2)
         nc.sync.dma_start(l_keys[:], offs)
-        for q in range(4):
-            nc.scalar.dma_start(ks[32 * q : 32 * q + 4, :].bitcast(I32), keys_scales[0, 4 * q : 4 * q + 4, :].bitcast(I32))
         for t in range(1, PACK):
             nc.sync.dma_start(npl[t][:], nv[:, t, :])
-        nc.sync.dma_start(kw[:], keys_words[0].rearrange("p n t -> p (n t)").bitcast(I32))
         nc.sync.dma_start(l_users[:], offs3)
-        nc.sync.dma_start(l_put[:], offs4)
         for t in range(PACK):
             nc.sync.dma_start(upl[t][:], uv[:, t, :])
+        nc.sync.dma_start(kw[:], keys_words[0].rearrange("p n t -> p (n t)").bitcast(I32))
+        nc.sync.dma_start(l_put[:], offs4)
         for r in range(TILES):
             nc.sync.dma_start(olds[r][:], old[r * P : (r + 1) * P, :])
 
-        def gather(engine, dst, plane, offsets):
-            if engine == "v":
-                nc.vector.tensor_copy(dst, plane[:].indirect(offsets))
-            else:
-                nc.scalar.activation(dst, plane[:].indirect(offsets), COPY)
+        codes = [sb.tile([P, J], U32, name="codes%d" % h, align_bytes=64) for h in range(2)]
+        planes = [sb.tile([P, J], U8, name="planes%d" % h, align_bytes=64) for h in range(2)]
+        kq_s = sb.tile([P, I], U8, name="kq_s", align_bytes=64)
+        picked = [sb.tile([P, PACK, J], BF16, name="picked%d" % s) for s in range(2)]
+        woven = [[sb.tile([P, HALF, PACK], BF16, name="woven%d_%d" % (s, h), align_bytes=64) for h in range(2)] for s in range(2)]
 
-        def weave(dst, src):
-            nc.vector.tensor_copy(
-                dst[:].rearrange("p (c i) t -> p c t i", i=4),
-                src.rearrange("p t (c i) -> p c t i", i=4),
+        def pick(s, t, loaded, offsets, share):
+            nc.vector.tensor_copy(picked[s][:, t, 0:share], loaded[:].indirect(offsets[:, 0 : share // 16]))
+            nc.scalar.activation(picked[s][:, t, share:J], loaded[:].indirect(offsets[:, share // 16 : J // 16]), COPY)
+
+        def weave(copy, s, h, lo, hi):
+            copy(
+                woven[s][h][:, lo:hi, :].rearrange("p (c i) t -> p c t i", i=4),
+                picked[s][:, :, h * HALF + lo : h * HALF + hi].rearrange("p t (c i) -> p c t i", i=4),
             )
 
-        ng = sb.tile([P, PACK, J], BF16, name="ng")
+        def quantize(s, h):
+            nc.vector.quantize_mx(
+                out=codes[h][:, s * HALF : (s + 1) * HALF].bitcast(FP8X4),
+                scales=planes[h][:, s * HALF : (s + 1) * HALF],
+                in_=woven[s][h][:].rearrange("p c t -> p (c t)"),
+            )
+
+        shares = [192,192,192,320,192,192,192,320]
         for t in range(PACK):
-            gather("vs"[t % 2], ng[:, t, :], npl[t], l_notes[:])
-        kq_s = sb.tile([P, I], U8, name="kq_s", align_bytes=64)
-        nc.vector.tensor_copy(kq_s[:], ks[:].indirect(l_keys[:]))
-        nw = sb.tile([P, J, PACK], BF16, name="nw", align_bytes=64)
-        weave(nw, ng[:])
-        nq = sb.tile([P, J], U32, name="nq", align_bytes=64)
-        nq_s = sb.tile([P, J], U8, name="nq_s", align_bytes=64)
-        nc.vector.quantize_mx(out=nq[:].bitcast(FP8X4), scales=nq_s[:], in_=nw[:].rearrange("p c t -> p (c t)"))
+            pick(0, t, npl[t], l_notes, shares[t])
+            if t == 1:
+                nc.vector.tensor_copy(kq_s[:], ks[:].indirect(l_keys[:]))
+        for h in range(2):
+            weave(nc.vector.tensor_copy, 0, h, 0, HALF)
+        for h in range(2):
+            quantize(0, h)
+        for t in range(PACK):
+            pick(1, t, upl[t], l_users, shares[PACK + t])
+        weave(nc.vector.tensor_copy, 1, 0, 0, HALF)
+        weave(nc.vector.tensor_copy, 1, 1, 0, 128)
+        weave(nc.scalar.copy, 1, 1, 128, HALF)
+        for h in range(2):
+            quantize(1, h)
 
         kq = [sb.tile([P, P], U32, name="kq%d" % r, align_bytes=64) for r in range(TILES)]
-        best = [sb.tile([P, 2, N], F32, name="best%d" % r) for r in range(TILES)]
-        g1 = [ps.tile([P, J], F32, name="g1_%d" % r) for r in range(TILES)]
-        g2 = [ps.tile([P, J], F32, name="g2_%d" % r) for r in range(TILES)]
+        banks = [[ps.tile([P, J], F32, name="bank%d_%d" % (r, h)) for h in range(2)] for r in range(TILES)]
         for r in range(TILES):
             nc.vector.tensor_copy(kq[r][:], kw[:].bitcast(U32).indirect(l_keys[:, 8 * r : 8 * r + 8]))
-            nc.tensor.matmul_mx(
-                out=g1[r][:], lhsT=kq[r][:].bitcast(FP8X4), lhsT_scale=kq_s[:, r * P : (r + 1) * P],
-                rhs=nq[:].bitcast(FP8X4), rhs_scale=nq_s[:], start=True, stop=True,
-            )
-        for r in range(TILES):
-            nc.vector.tensor_reduce(best[r][:, 0, :], g1[r][:].rearrange("p (n e) -> p n e", e=RUN), AXIS_X, MAX)
-
-        ug = sb.tile([P, PACK, J], BF16, name="ug")
-        for t in range(PACK - 1):
-            gather("s", ug[:, t, :], upl[t], l_users[:])
-        gather("v", ug[:, 3, 0:HALF], upl[3], l_users[:, 0:16])
-        gather("s", ug[:, 3, HALF:J], upl[3], l_users[:, 16:32])
-        uw = [sb.tile([P, HALF, PACK], BF16, name="uw%d" % h, align_bytes=64) for h in range(2)]
-        uq = [sb.tile([P, HALF], U32, name="uq%d" % h, align_bytes=64) for h in range(2)]
-        uq_s = [sb.tile([P, HALF], U8, name="uq_s%d" % h, align_bytes=64) for h in range(2)]
-        for h in range(2):
-            weave(uw[h], ug[:, :, h * HALF : (h + 1) * HALF])
-        for h in range(2):
-            nc.vector.quantize_mx(out=uq[h][:].bitcast(FP8X4), scales=uq_s[h][:], in_=uw[h][:].rearrange("p c t -> p (c t)"))
-        for r in range(TILES):
             for h in range(2):
                 nc.tensor.matmul_mx(
-                    out=g2[r][:, h * HALF : (h + 1) * HALF], lhsT=kq[r][:].bitcast(FP8X4), lhsT_scale=kq_s[:, r * P : (r + 1) * P],
-                    rhs=uq[h][:].bitcast(FP8X4), rhs_scale=uq_s[h][:], start=True, stop=True,
+                    out=banks[r][h][:], lhsT=kq[r][:].bitcast(FP8X4), lhsT_scale=kq_s[:, r * P : (r + 1) * P],
+                    rhs=codes[h][:].bitcast(FP8X4), rhs_scale=planes[h][:], start=True, stop=True,
                 )
 
         rb = [sb.tile([P, N], F32, name="rb%d" % r) for r in range(TILES)]
         res = [sb.tile([P, M], F32, name="res%d" % r) for r in range(TILES)]
-
-        def finish(r):
-            nc.vector.tensor_reduce(rb[r][:], best[r][:].rearrange("p s n -> p n s"), AXIS_X, MAX)
+        for r in range(TILES):
+            for h in range(2):
+                nc.vector.tensor_reduce(
+                    rb[r][:, h * (N // 2) : (h + 1) * (N // 2)],
+                    banks[r][h][:].rearrange("p (s n e) -> p n s e", s=2, e=RUN), AXIS_XY, MAX,
+                )
             nc.scalar.activation(puts[r][:].indirect(l_put[:]), rb[r][:], COPY)
-
+        pool_cols = [512,512,0,0]
         for r in range(TILES):
-            nc.vector.tensor_reduce(best[r][:, 1, :], g2[r][:].rearrange("p (n e) -> p n e", e=RUN), AXIS_X, MAX)
-            if r > 0:
-                finish(r - 1)
-        finish(TILES - 1)
-        for r in range(TILES):
-            nc.vector.tensor_tensor(res[r][:], puts[r][:], olds[r][:], ADD)
+            c = pool_cols[r]
+            if c > 0:
+                nc.gpsimd.tensor_tensor(res[r][:, 0:c], puts[r][:, 0:c], olds[r][:, 0:c], ADD)
+            if c < M:
+                nc.vector.tensor_tensor(res[r][:, c:M], puts[r][:, c:M], olds[r][:, c:M], ADD)
             nc.sync.dma_start(out[r * P : (r + 1) * P, :], res[r][:])

@@ -41,22 +41,25 @@ def tile_attend_tab_larger_runsput_kernel(tc, keys_words, keys_scales, notes, us
         olds = [sb.tile([P, M], F32, name="old%d" % r) for r in range(TILES)]
         puts = [sb.tile([P, M], F32, name="put%d" % r) for r in range(TILES)]
 
-        nc.gpsimd.memset(ks[:].bitcast(I32), 0)
-        for q in range(4):
-            nc.gpsimd.dma_start(ks[32 * q : 32 * q + 4, :].bitcast(I32), keys_scales[0, 4 * q : 4 * q + 4, :].bitcast(I32))
+        nc.vector.memset(ks[:].bitcast(I32), 0)
         for r in range(TILES):
-            nc.gpsimd.memset(puts[r][:], 0.0)
+            nc.vector.memset(puts[r][:], 0.0)
 
         nv = notes.rearrange("(p t) u -> p t u", t=PACK)
         uv = users2.rearrange("(p t) u -> p t u", t=PACK)
         nc.sync.dma_start(npl[0][:], nv[:, 0, :])
         nc.sync.dma_start(l_notes[:], offs2)
+        nc.sync.dma_start(npl[1][:], nv[:, 1, :])
+        for q in range(4):
+            nc.sync.dma_start(ks[32 * q : 32 * q + 4, :].bitcast(I32), keys_scales[0, 4 * q : 4 * q + 4, :].bitcast(I32))
+        nc.sync.dma_start(npl[2][:], nv[:, 2, :])
         nc.sync.dma_start(l_keys[:], offs)
-        for t in range(1, PACK):
-            nc.sync.dma_start(npl[t][:], nv[:, t, :])
+        nc.sync.dma_start(npl[3][:], nv[:, 3, :])
         nc.sync.dma_start(l_users[:], offs3)
-        for t in range(PACK):
-            nc.sync.dma_start(upl[t][:], uv[:, t, :])
+        nc.sync.dma_start(upl[0][:], uv[:, 0, :])
+        nc.sync.dma_start(upl[1][:], uv[:, 1, :])
+        nc.sync.dma_start(upl[2][:], uv[:, 2, :])
+        nc.sync.dma_start(upl[3][:], uv[:, 3, :])
         nc.sync.dma_start(kw[:], keys_words[0].rearrange("p n t -> p (n t)").bitcast(I32))
         nc.sync.dma_start(l_put[:], offs4)
         for r in range(TILES):
@@ -85,27 +88,27 @@ def tile_attend_tab_larger_runsput_kernel(tc, keys_words, keys_scales, notes, us
                 in_=woven[s][h][:].rearrange("p c t -> p (c t)"),
             )
 
-        shares = [192,192,192,320,192,192,192,320]
+        shares = [0,0,0,0,128,128,128,256]
         for t in range(PACK):
-            pick(0, t, npl[t], l_notes, shares[t])
-            if t == 1:
-                nc.vector.tensor_copy(kq_s[:], ks[:].indirect(l_keys[:]))
-        for h in range(2):
-            weave(nc.vector.tensor_copy, 0, h, 0, HALF)
+            nc.vector.tensor_copy(woven[0][0][:, :, t], npl[t][:].indirect(l_notes[:, 0:16]))
+            nc.scalar.activation(picked[0][:, t, HALF:J], npl[t][:].indirect(l_notes[:, 16:32]), COPY)
+        weave(nc.vector.tensor_copy, 0, 1, 0, HALF)
         for h in range(2):
             quantize(0, h)
+        nc.vector.tensor_copy(kq_s[:], ks[:].indirect(l_keys[:]))
         for t in range(PACK):
             pick(1, t, upl[t], l_users, shares[PACK + t])
         weave(nc.vector.tensor_copy, 1, 0, 0, HALF)
-        weave(nc.vector.tensor_copy, 1, 1, 0, 128)
-        weave(nc.scalar.copy, 1, 1, 128, HALF)
-        for h in range(2):
-            quantize(1, h)
+        weave(nc.scalar.copy, 1, 1, 0, HALF)
+        quantize(1, 0)
 
         kq = [sb.tile([P, P], U32, name="kq%d" % r, align_bytes=64) for r in range(TILES)]
         banks = [[ps.tile([P, J], F32, name="bank%d_%d" % (r, h)) for h in range(2)] for r in range(TILES)]
         for r in range(TILES):
             nc.vector.tensor_copy(kq[r][:], kw[:].bitcast(U32).indirect(l_keys[:, 8 * r : 8 * r + 8]))
+            if r == 3:
+                quantize(1, 1)
+        for r in range(TILES):
             for h in range(2):
                 nc.tensor.matmul_mx(
                     out=banks[r][h][:], lhsT=kq[r][:].bitcast(FP8X4), lhsT_scale=kq_s[:, r * P : (r + 1) * P],
@@ -126,6 +129,12 @@ def tile_attend_tab_larger_runsput_kernel(tc, keys_words, keys_scales, notes, us
             c = pool_cols[r]
             if c > 0:
                 nc.gpsimd.tensor_tensor(res[r][:, 0:c], puts[r][:, 0:c], olds[r][:, 0:c], ADD)
-            if c < M:
+            if c < M and r < TILES - 1:
                 nc.vector.tensor_tensor(res[r][:, c:M], puts[r][:, c:M], olds[r][:, c:M], ADD)
-            nc.sync.dma_start(out[r * P : (r + 1) * P, :], res[r][:])
+            if r < TILES - 1:
+                nc.sync.dma_start(out[r * P : (r + 1) * P, :], res[r][:])
+            else:
+                for lo in (0, M // 2):
+                    hi = lo + M // 2
+                    nc.vector.tensor_tensor(res[r][:, lo:hi], puts[r][:, lo:hi], olds[r][:, lo:hi], ADD)
+                    nc.sync.dma_start(out[r * P : (r + 1) * P, lo:hi], res[r][:, lo:hi])

@@ -50,8 +50,8 @@ def tile_attend_tab_larger_runsput_kernel(tc, keys_words, keys_scales, notes, us
         nc.sync.dma_start(npl[0][:], nv[:, 0, :])
         nc.sync.dma_start(l_notes[:], offs2)
         nc.sync.dma_start(npl[1][:], nv[:, 1, :])
-        for q in range(4):
-            nc.sync.dma_start(ks[32 * q : 32 * q + 4, :].bitcast(I32), keys_scales[0, 4 * q : 4 * q + 4, :].bitcast(I32))
+        for f in range(4):
+            nc.sync.dma_start(ks[f:P:32, :].bitcast(I32), keys_scales[0, f:16:4, :].bitcast(I32))
         nc.sync.dma_start(npl[2][:], nv[:, 2, :])
         nc.sync.dma_start(l_keys[:], offs)
         nc.sync.dma_start(npl[3][:], nv[:, 3, :])

from contextlib import ExitStack

import concourse.mybir as mybir

D, T, I, J, U, M, N = 512, 2048, 512, 512, 1024, 512, 64
FLOPS = 2 * 2 * D * I * J

F32 = mybir.dt.float32
BF16 = mybir.dt.bfloat16
I32 = mybir.dt.int32
U32 = mybir.dt.uint32
U16 = mybir.dt.uint16
U8 = mybir.dt.uint8
FP8X4 = mybir.dt.float8_e4m3fn_x4
COPY = mybir.ActivationFunctionType.Copy
MAX = mybir.AluOpType.max
ADD = mybir.AluOpType.add
AXIS_XY = mybir.AxisListType.XY

P = 128
PACK = 4
RUN = J // N
TILES = I // P
HALF = J // 2


def tile_attend_tab_larger_runsput_kernel(tc, keys_words, keys_scales, notes, users2, old, offs, offs2, offs3, offs4, out):
    nc = tc.nc
    with ExitStack() as ctx:
        sb = ctx.enter_context(tc.tile_pool(name="sb", bufs=1))
        ps = ctx.enter_context(tc.psum_pool(name="ps", bufs=1))

        l_keys = sb.tile([P, I // 16], U16, name="l_keys")
        l_notes = sb.tile([P, J // 16], U16, name="l_notes")
        l_users = sb.tile([P, J // 16], U16, name="l_users")
        l_put = sb.tile([P, N // 16], U16, name="l_put")
        kw = sb.tile([P, T], I32, name="kw")
        ks = sb.tile([P, T], U8, name="ks")
        npl = [sb.tile([P, U], F32, name="npl%d" % t) for t in range(PACK)]
        upl = [sb.tile([P, U], F32, name="upl%d" % t) for t in range(PACK)]
        olds = [sb.tile([P, M], F32, name="old%d" % r) for r in range(TILES)]
        puts = [sb.tile([P, M], F32, name="put%d" % r) for r in range(TILES)]

        nc.vector.memset(ks[:].bitcast(I32), 0)
        for r in range(TILES):
            nc.vector.memset(puts[r][:], 0.0)

        nv = notes.rearrange("(p t) u -> p t u", t=PACK)
        uv = users2.rearrange("(p t) u -> p t u", t=PACK)
        nc.sync.dma_start(npl[0][:], nv[:, 0, :])
        nc.sync.dma_start(l_notes[:], offs2)
        nc.sync.dma_start(npl[1][:], nv[:, 1, :])
        for f in range(4):
            nc.sync.dma_start(ks[f:P:32, :].bitcast(I32), keys_scales[0, f:16:4, :].bitcast(I32))
        nc.sync.dma_start(npl[2][:], nv[:, 2, :])
        nc.sync.dma_start(l_keys[:], offs)
        nc.sync.dma_start(npl[3][:], nv[:, 3, :])
        nc.sync.dma_start(l_users[:], offs3)
        nc.sync.dma_start(upl[0][:], uv[:, 0, :])
        nc.sync.dma_start(upl[1][:], uv[:, 1, :])
        nc.sync.dma_start(upl[2][:], uv[:, 2, :])
        nc.sync.dma_start(upl[3][:], uv[:, 3, :])
        nc.sync.dma_start(kw[:], keys_words[0].rearrange("p n t -> p (n t)").bitcast(I32))
        nc.sync.dma_start(l_put[:], offs4)
        for r in range(TILES):
            nc.sync.dma_start(olds[r][:], old[r * P : (r + 1) * P, :])

        codes = [sb.tile([P, J], U32, name="codes%d" % h, align_bytes=64) for h in range(2)]
        planes = [sb.tile([P, J], U8, name="planes%d" % h, align_bytes=64) for h in range(2)]
        kq_s = sb.tile([P, I], U8, name="kq_s", align_bytes=64)
        picked = [sb.tile([P, PACK, J], BF16, name="picked%d" % s) for s in range(2)]
        woven = [[sb.tile([P, HALF, PACK], BF16, name="woven%d_%d" % (s, h), align_bytes=64) for h in range(2)] for s in range(2)]

        def pick(s, t, loaded, offsets, share):
            nc.vector.tensor_copy(picked[s][:, t, 0:share], loaded[:].indirect(offsets[:, 0 : share // 16]))
            nc.scalar.activation(picked[s][:, t, share:J], loaded[:].indirect(offsets[:, share // 16 : J // 16]), COPY)

        def weave(copy, s, h, lo, hi):
            copy(
                woven[s][h][:, lo:hi, :].rearrange("p (c i) t -> p c t i", i=4),
                picked[s][:, :, h * HALF + lo : h * HALF + hi].rearrange("p t (c i) -> p c t i", i=4),
            )

        def quantize(s, h):
            nc.vector.quantize_mx(
                out=codes[h][:, s * HALF : (s + 1) * HALF].bitcast(FP8X4),
                scales=planes[h][:, s * HALF : (s + 1) * HALF],
                in_=woven[s][h][:].rearrange("p c t -> p (c t)"),
            )

        shares = [0,0,0,0,128,128,128,256]
        for t in range(PACK):
            nc.vector.tensor_copy(woven[0][0][:, :, t], npl[t][:].indirect(l_notes[:, 0:16]))
            nc.scalar.activation(picked[0][:, t, HALF:J], npl[t][:].indirect(l_notes[:, 16:32]), COPY)
        weave(nc.vector.tensor_copy, 0, 1, 0, HALF)
        for h in range(2):
            quantize(0, h)
        nc.vector.tensor_copy(kq_s[:], ks[:].indirect(l_keys[:]))
        for t in range(PACK):
            pick(1, t, upl[t], l_users, shares[PACK + t])
        weave(nc.vector.tensor_copy, 1, 0, 0, HALF)
        weave(nc.scalar.copy, 1, 1, 0, HALF)
        quantize(1, 0)

        kq = [sb.tile([P, P], U32, name="kq%d" % r, align_bytes=64) for r in range(TILES)]
        banks = [[ps.tile([P, J], F32, name="bank%d_%d" % (r, h)) for h in range(2)] for r in range(TILES)]
        for r in range(TILES):
            nc.vector.tensor_copy(kq[r][:], kw[:].bitcast(U32).indirect(l_keys[:, 8 * r : 8 * r + 8]))
            if r == 3:
                quantize(1, 1)
        for r in range(TILES):
            for h in range(2):
                nc.tensor.matmul_mx(
                    out=banks[r][h][:], lhsT=kq[r][:].bitcast(FP8X4), lhsT_scale=kq_s[:, r * P : (r + 1) * P],
                    rhs=codes[h][:].bitcast(FP8X4), rhs_scale=planes[h][:], start=True, stop=True,
                )

        rb = [sb.tile([P, N], F32, name="rb%d" % r) for r in range(TILES)]
        res = [sb.tile([P, M], F32, name="res%d" % r) for r in range(TILES)]
        for r in range(TILES):
            for h in range(2):
                nc.vector.tensor_reduce(
                    rb[r][:, h * (N // 2) : (h + 1) * (N // 2)],
                    banks[r][h][:].rearrange("p (s n e) -> p n s e", s=2, e=RUN), AXIS_XY, MAX,
                )
            nc.scalar.activation(puts[r][:].indirect(l_put[:]), rb[r][:], COPY)
        pool_cols = [512,512,0,0]
        for r in range(TILES):
            c = pool_cols[r]
            if c > 0:
                nc.gpsimd.tensor_tensor(res[r][:, 0:c], puts[r][:, 0:c], olds[r][:, 0:c], ADD)
            if c < M and r < TILES - 1:
                nc.vector.tensor_tensor(res[r][:, c:M], puts[r][:, c:M], olds[r][:, c:M], ADD)
            if r < TILES - 1:
                nc.sync.dma_start(out[r * P : (r + 1) * P, :], res[r][:])
            else:
                for lo in (0, M // 2):
                    hi = lo + M // 2
                    nc.vector.tensor_tensor(res[r][:, lo:hi], puts[r][:, lo:hi], olds[r][:, lo:hi], ADD)
                    nc.sync.dma_start(out[r * P : (r + 1) * P, lo:hi], res[r][:, lo:hi])
